import numpy as np
import ml_dtypes


def mxq(x, axis, fmt="e4m3"):
    dtype, down = {"e4m3": (ml_dtypes.float8_e4m3fn, 7), "e5m2": (ml_dtypes.float8_e5m2, 14)}[fmt]
    v = np.moveaxis(np.asarray(x, np.float32).astype(ml_dtypes.bfloat16).astype(np.float64), axis, -1)
    blocks = v.reshape(v.shape[:-1] + (-1, 32))
    amax = np.abs(blocks).max(-1, keepdims=True)
    byte = np.maximum(np.where(amax > 0, np.frexp(amax)[1] - 1 + 127, 0) - down, 1)
    scale = np.exp2(byte - 127.0)
    codes = (blocks / scale).astype(np.float32).astype(dtype).astype(np.float64)
    return np.moveaxis((codes * scale).reshape(v.shape), -1, axis)


WIDE = False


def mx_kscale(k):
    if not WIDE:
        return np.ones(k)
    levels = np.array([10, -10, 5, -5, 0])
    if k % 512:
        return np.exp2(np.random.permutation(np.resize(levels, k // 32))).repeat(32)
    a = np.empty((k // 512, 16))
    for p in range(k // 512):
        a[p, :8] = np.random.permutation(np.resize(levels, 8))
        for g in range(8):
            far = levels[np.abs(levels - a[p, g]) >= 10]
            a[p, g + 8] = far[np.random.randint(len(far))]
    return np.exp2(a.ravel()).repeat(32)


def f64(x):
    return np.asarray(x).astype(np.float64)


def striped(idx):
    return np.tile(idx.reshape(-1, 16).T, (8, 1)).astype(np.uint16)


def unstriped(offs):
    return offs[:16].T.reshape(-1).astype(np.int64)


def striped8(idx):
    return np.concatenate([x.reshape(-1, 16).T for x in idx]).astype(np.uint16)


def runs(offs, k):
    lists = np.stack([offs[16 * r : 16 * r + 16].T.reshape(-1) for r in range(8)]).astype(np.int64)
    return lists[np.arange(k) % 512 // 64]


def pack_weight(w):
    k, n = w.shape
    w = f64(np.asarray(w, np.float32).astype(ml_dtypes.bfloat16)).reshape(k // 32, 32, n)
    amax = np.abs(w).max(1)
    byte = np.clip(np.where(amax > 0, np.frexp(amax)[1] - 1 + 127 - 7, 1), 1, 254)
    scaled = (w * np.exp2(127.0 - byte)[:, None, :]).reshape(k, n).astype(np.float32)
    words = np.ascontiguousarray(scaled.reshape(k // 512, 128, 4, n).transpose(0, 1, 3, 2)).astype(ml_dtypes.float8_e4m3fn).view(np.uint8)
    return words, np.ascontiguousarray(byte.astype(np.uint8).reshape(k // 512, 16, n))


def unpack_weight(words, scales):
    g, p, n, _ = words.shape
    vals = np.ascontiguousarray(words).view(ml_dtypes.float8_e4m3fn).astype(np.float64) * np.repeat(np.exp2(scales.astype(np.float64) - 127.0), 8, axis=1)[..., None]
    return vals.transpose(0, 1, 3, 2).reshape(g * 512, n)


def sigmoid(v):
    return 1.0 / (1.0 + np.exp(-np.maximum(v, -700.0)))

def planes(y):
    n, m = y.shape
    v = y.astype(np.float32).astype(ml_dtypes.bfloat16).astype(np.float64).reshape(n // 32, 32, m)
    top = np.abs(v).max(1)
    byte = np.clip(np.where(top > 0, np.frexp(top)[1] - 1 + 127 - 7, 1), 1, 254)
    codes = (v * np.exp2(127.0 - byte)[:, None, :]).reshape(n, m).astype(np.float32).astype(ml_dtypes.float8_e4m3fn).view(np.uint8)
    words = codes.reshape(n // 512, 128, 4, m).transpose(0, 1, 3, 2)
    return np.ascontiguousarray(words), np.ascontiguousarray(byte.astype(np.uint8).reshape(n // 512, 16, m))


K, T, S, N, G, H, W = 512, 1024, 256, 512, 2048, 512, 128


def setup_inputs():
    n = np.random.standard_normal
    s = mx_kscale(K)[:, None]
    u = mx_kscale(K)
    packed_xT = pack_weight(n((K, T)) * s)
    packed_dT = pack_weight(n((K, G)) / s)
    packed_w1 = pack_weight(n((H, N)) / np.sqrt(2 * H) / u[:, None])
    packed_w2 = pack_weight(n((H, N)) / np.sqrt(2 * H) / u[:, None])
    perm = np.random.permutation(S)
    return {
        "x_words": packed_xT[0],
        "x_scales": packed_xT[1],
        "d_words": packed_dT[0],
        "d_scales": packed_dT[1],
        "sl": np.random.uniform(1.0, 2.0, (H, 1)).astype(np.float32),
        "th": (0.5 * n((H, 1))).astype(np.float32),
        "tau": np.random.uniform(0.2, 0.6, (H, 1)).astype(np.float32),
        "tau2": np.random.uniform(0.6, 1.0, (H, 1)).astype(np.float32),
        "gn": (np.random.uniform(0.5, 1.5, (H, 1)) * u[:, None]).astype(np.float32),
        "gm": (np.random.uniform(0.5, 1.5, (H, 1)) * u[:, None]).astype(np.float32),
        "w1_words": packed_w1[0],
        "w1_scales": packed_w1[1],
        "w2_words": packed_w2[0],
        "w2_scales": packed_w2[1],
        "sl2": np.random.uniform(1.0, 2.0, (N, 1)).astype(np.float32),
        "th2": (0.5 * n((N, 1))).astype(np.float32),
        "offs": striped(np.random.permutation(T)[:S]),
        "k1": striped8(np.random.randint(0, G, (8, H))),
        "two": striped(np.random.permutation(T)[:S]),
        "k2": striped8(np.random.randint(0, G, (8, H))),
        "n1": striped(perm[:W]),
        "n2": striped(perm[W:]),
        "n3": striped(np.random.permutation(S)),
        "n4": striped(np.random.permutation(S)),
        "n5": striped(np.random.permutation(S)),
        "n6": striped(np.random.permutation(S)),
    }


def reference(x_words, x_scales, d_words, d_scales, sl, th, tau, tau2, gn, gm, w1_words, w1_scales, w2_words, w2_scales, sl2, th2, offs, k1, two, k2, n1, n2, n3, n4, n5, n6):
    d_k1 = unpack_weight(d_words, d_scales)[np.arange(K)[:, None], runs(k1, K)]
    xq = unpack_weight(x_words, x_scales)[:, unstriped(offs)]
    a = 0.0625 * (d_k1.T @ xq)
    pb = a[:, unstriped(n2)]
    sg = sigmoid(f64(sl) * (a[:, unstriped(n1)] - f64(th)))
    rb = pb - sg
    pa = a[:, unstriped(n1)]
    sg2 = sigmoid(f64(sl) * (a[:, unstriped(n2)] - f64(th)))
    ra = pa * sg2
    ds = np.zeros((H, S))
    ds[:, unstriped(n1)] = ra
    dt = ds.copy()
    dt[:, unstriped(n2)] = rb
    z = f64(gn) * dt
    d_k2 = unpack_weight(d_words, d_scales)[np.arange(K)[:, None], runs(k2, K)]
    x_two = unpack_weight(x_words, x_scales)[:, unstriped(two)]
    b = 0.0625 * (d_k2.T @ x_two)
    top = b.max(axis=1, keepdims=True)
    ea = np.exp(f64(tau) * (b[:, unstriped(n3)] - top))
    ea2 = np.exp(f64(tau2) * (b[:, unstriped(n4)] - top))
    z2 = f64(gm) * (3.0 * (ea - ea2))
    h = unpack_weight(w1_words, w1_scales).T @ mxq(z, 0, "e4m3") + unpack_weight(w2_words, w2_scales).T @ mxq(z2, 0, "e4m3")
    sg3 = sigmoid(f64(sl2) * (h[:, unstriped(n6)] - f64(th2)))
    out_0 = h + sg3 * (h[:, unstriped(n5)] - h)
    return (out_0,) + planes(out_0)

@@ -1,0 +1,261 @@
+from contextlib import ExitStack
+
+import concourse.mybir as mybir
+
+F32 = mybir.dt.float32
+BF16 = mybir.dt.bfloat16
+I32 = mybir.dt.int32
+U32 = mybir.dt.uint32
+U16 = mybir.dt.uint16
+U8 = mybir.dt.uint8
+FP8X4 = mybir.dt.float8_e4m3fn_x4
+ALU = mybir.AluOpType
+ACT = mybir.ActivationFunctionType
+
+P = 128
+PACK = 4
+TOKENS = 1024
+CODEWORDS = 2048
+FEATURES = 512
+PLACES = 256
+PAIRS = 128
+WIDE = 2 * PLACES
+FLOPS = 4 * 2 * 512 * 512 * 256
+
+
+def tile_picked_pqjeodetwetr_none_po_kernel(
+    tc, x_words, x_scales, d_words, d_scales, sl, th, tau, tau2, gn, gm, w1_words, w1_scales, w2_words, w2_scales,
+    sl2, th2, offs, k1, two, k2, n1, n2, n3, n4, n5, n6, out_0, out_1, out_2,
+):
+    nc = tc.nc
+    with ExitStack() as ctx:
+        sb = ctx.enter_context(tc.tile_pool(name="sb", bufs=1))
+        ps = ctx.enter_context(tc.psum_pool(name="ps", bufs=1))
+
+        def tile(name, shape, dtype, tag=None):
+            return sb.tile(shape, dtype, name=name, tag=tag or name, align_bytes=64)
+
+        def load_list(name, src):
+            held = tile(name, list(src.shape), U16)
+            nc.sync.dma_start(held[:], src)
+            return held
+
+        def load_words(name, src, tag):
+            held = tile(name, [P, src.shape[2]], U32, tag)
+            nc.sync.dma_start(held[:].bitcast(I32), src[0].rearrange("p c r -> p (c r)").bitcast(I32))
+            return held
+
+        def load_scale_table(name, src):
+            width = src.shape[2]
+            held = tile(name, [P, width], U8)
+            nc.sync.dma_start(held[:].bitcast(I32), src[0].bitcast(I32).unsqueeze(1).broadcast_to([16, 8, width // 4]))
+            return held
+
+        def load_rows(name, src):
+            held = tile(name, [P, PACK], F32)
+            nc.gpsimd.dma_start(held[:], src.rearrange("(p t) o -> p (t o)", t=PACK))
+            return held
+
+        def sigmoid_bias(name, slope, threshold):
+            negated = tile(name + "_neg", [P, PACK], F32)
+            bias = tile(name, [P, PACK], F32)
+            nc.gpsimd.tensor_scalar(negated[:], threshold[:], -1.0, 0.0, ALU.mult, ALU.add)
+            nc.gpsimd.tensor_tensor(bias[:], slope[:], negated[:], ALU.mult)
+            return bias
+
+        def zeroed_bytes(engine, name, width, tag=None):
+            held = tile(name, [P, width], U8, tag)
+            engine.memset(held[:].bitcast(I32), 0)
+            return held
+
+        def deal(dst, src):
+            nc.vector.tensor_copy(dst.rearrange("p (t m) -> p m t", t=PACK), src.rearrange("p (m t) -> p m t", t=PACK))
+
+        def gather(dst, window, offsets):
+            nc.vector.tensor_copy(dst, window[:].indirect(offsets[:]))
+
+        def move_scale_rows(queue, plane, staged):
+            for r in range(4):
+                queue.dma_start(plane[r:P:32, :].bitcast(I32), staged[8 * r : P : 32, :].bitcast(I32))
+
+        def product(bank, words, scales, t, rhs, rhs_scales, start, stop):
+            cols = slice(P * t, P * (t + 1))
+            nc.tensor.matmul_mx(
+                out=bank[:], lhsT=words[:, cols].bitcast(FP8X4), lhsT_scale=scales[:, cols],
+                rhs=rhs.bitcast(FP8X4), rhs_scale=rhs_scales, start=start, stop=stop,
+            )
+
+        two_t = load_list("two_t", two)
+        x_bytes = load_scale_table("x_bytes", x_scales)
+        k2_t = load_list("k2_t", k2)
+        d_bytes = load_scale_table("d_bytes", d_scales)
+        x_table = load_words("x_table", x_words, "x_table")
+        d_table = load_words("d_table", d_words, "d_table")
+        k1_t = load_list("k1_t", k1)
+        offs_t = load_list("offs_t", offs)
+        n3_t = load_list("n3_t", n3)
+        n4_t = load_list("n4_t", n4)
+        n1_t = load_list("n1_t", n1)
+        n2_t = load_list("n2_t", n2)
+        n5_t = load_list("n5_t", n5)
+        n6_t = load_list("n6_t", n6)
+        tau_t = load_rows("tau_t", tau)
+        tau2_t = load_rows("tau2_t", tau2)
+        sl_t = load_rows("sl_t", sl)
+        th_t = load_rows("th_t", th)
+        gm_t = load_rows("gm_t", gm)
+        gn_t = load_rows("gn_t", gn)
+        sl2_t = load_rows("sl2_t", sl2)
+        th2_t = load_rows("th2_t", th2)
+        bias_s = sigmoid_bias("bias_s", sl_t, th_t)
+        bias_s3 = sigmoid_bias("bias_s3", sl2_t, th2_t)
+        plane_b = zeroed_bytes(nc.vector, "plane_b", FEATURES + PLACES, "reuse_plane")
+        plane_a = zeroed_bytes(nc.vector, "plane_a", FEATURES + PLACES)
+
+        db_b = tile("db_b", [P, FEATURES], U8)
+        xb_b = tile("xb_b", [P, PLACES], U8)
+        staged_b = tile("staged_b", [P, FEATURES + PLACES], U8)
+        gather(xb_b[:], x_bytes, two_t)
+        gather(db_b[:], d_bytes, k2_t)
+        nc.vector.tensor_copy(staged_b[:, FEATURES:].bitcast(I32), xb_b[:].bitcast(I32))
+        deal(staged_b[:, 0:FEATURES], db_b[:])
+        move_scale_rows(nc.scalar, plane_b, staged_b)
+        xw_b = tile("xw_b", [P, PLACES], U32, "reuse_x")
+        dw_b = tile("dw_b", [P, FEATURES], U32, "reuse_raw")
+        dealt_b = tile("dealt_b", [P, FEATURES], U32, "reuse_dealt")
+        gather(xw_b[:], x_table, two_t)
+        gather(dw_b[:], d_table, k2_t)
+        deal(dealt_b[:], dw_b[:])
+        b_banks = [ps.tile([P, PLACES], F32, name="b_bank%d" % t, tag="left%d" % t) for t in range(PACK)]
+        for t in range(PACK):
+            product(b_banks[t], dealt_b, plane_b, t, xw_b[:], plane_b[:, FEATURES:], True, True)
+
+        db_a = tile("db_a", [P, FEATURES], U8, "reuse_raw")
+        gather(db_a[:], d_bytes, k1_t)
+
+        b_rows = [tile("b_row%d" % t, [P, WIDE], F32) for t in range(PACK)]
+        top = tile("top", [P, PACK], F32)
+        bias_e = tile("bias_e", [P, PACK], F32)
+        bias_e2 = tile("bias_e2", [P, PACK], F32)
+        ea = tile("ea", [P, PACK, PLACES], F32)
+        ea2 = tile("ea2", [P, PACK, PLACES], F32)
+
+        def exponentials(t):
+            col = slice(t, t + 1)
+            nc.vector.tensor_scalar(b_rows[t][:, 0:PLACES], b_banks[t][:], 0.0625, None, ALU.mult, ALU.max, accum_out=top[:, col])
+            nc.vector.tensor_scalar(bias_e[:, col], top[:, col], tau_t[:, col], -1.0, ALU.mult, ALU.mult)
+            nc.vector.tensor_scalar(bias_e2[:, col], top[:, col], tau2_t[:, col], -1.0, ALU.mult, ALU.mult)
+            nc.scalar.activation(ea[:, t, :], b_rows[t][:].indirect(n3_t[:]), ACT.Exp, bias=bias_e[:, col], scale=tau_t[:, col])
+            nc.scalar.activation(ea2[:, t, :], b_rows[t][:].indirect(n4_t[:]), ACT.Exp, bias=bias_e2[:, col], scale=tau2_t[:, col])
+
+        exponentials(0)
+        exponentials(1)
+        xb_a = tile("xb_a", [P, PLACES], U8, "reuse_x")
+        staged_a = tile("staged_a", [P, FEATURES + PLACES], U8)
+        gather(xb_a[:], x_bytes, offs_t)
+        deal(staged_a[:, 0:FEATURES], db_a[:])
+        nc.vector.tensor_copy(staged_a[:, FEATURES:].bitcast(I32), xb_a[:].bitcast(I32))
+        move_scale_rows(nc.sync, plane_a, staged_a)
+        exponentials(2)
+        exponentials(3)
+
+        xw_a = tile("xw_a", [P, PLACES], U32, "reuse_plane")
+        dw_a = tile("dw_a", [P, FEATURES], U32, "reuse_dealt")
+        dealt_a = tile("dealt_a", [P, FEATURES], U32, "reuse_a")
+        gather(xw_a[:], x_table, offs_t)
+        gather(dw_a[:], d_table, k1_t)
+        deal(dealt_a[:], dw_a[:])
+        a_banks = [ps.tile([P, PLACES], F32, name="a_bank%d" % t, tag="right%d" % t) for t in range(PACK)]
+        for t in range(PACK):
+            product(a_banks[t], dealt_a, plane_a, t, xw_a[:], plane_a[:, FEATURES:], True, True)
+
+
+        a_rows = [tile("a_row%d" % t, [P, PLACES], F32) for t in range(PACK)]
+        sg = tile("sg", [P, PACK, PAIRS], F32)
+        sg2 = tile("sg2", [P, PACK, PAIRS], F32)
+        pa = tile("pa", [P, PACK, PAIRS], F32)
+        pb = tile("pb", [P, PACK, PAIRS], F32)
+        ra = tile("ra", [P, PACK, PAIRS], F32)
+        rb = tile("rb", [P, PACK, PAIRS], F32)
+        for t in range(PACK):
+            col = slice(t, t + 1)
+            nc.vector.tensor_scalar(a_rows[t][:], a_banks[t][:], 0.0625, None, ALU.mult)
+            nc.scalar.activation(sg2[:, t, :], a_rows[t][:].indirect(n2_t[:]), ACT.Sigmoid, bias=bias_s[:, col], scale=sl_t[:, col])
+            nc.scalar.activation(pa[:, t, :], a_rows[t][:].indirect(n1_t[:]), ACT.Copy)
+            nc.scalar.activation(sg[:, t, :], a_rows[t][:].indirect(n1_t[:]), ACT.Sigmoid, bias=bias_s[:, col], scale=sl_t[:, col])
+            nc.scalar.activation(pb[:, t, :], a_rows[t][:].indirect(n2_t[:]), ACT.Copy)
+        for t in range(PACK):
+            nc.vector.tensor_tensor(ra[:, t, :], pa[:, t, :], sg2[:, t, :], ALU.mult)
+            nc.vector.tensor_tensor(rb[:, t, :], pb[:, t, :], sg[:, t, :], ALU.subtract)
+
+        dt_rows = [tile("dt_row%d" % t, [P, PLACES], F32) for t in range(PACK)]
+        z_in = tile("z_in", [P, PLACES, PACK], BF16)
+        nc.scalar.activation(dt_rows[0][:].indirect(n1_t[:]), ra[:, 0, :], ACT.Copy)
+        for t in range(PACK):
+            if t + 1 < PACK:
+                nc.scalar.activation(dt_rows[t + 1][:].indirect(n1_t[:]), ra[:, t + 1, :], ACT.Copy)
+            nc.scalar.activation(dt_rows[t][:].indirect(n2_t[:]), rb[:, t, :], ACT.Copy)
+            nc.vector.tensor_scalar(z_in[:, :, t], dt_rows[t][:], gn_t[:, t : t + 1], None, ALU.mult)
+
+        diff = tile("diff", [P, PACK, PLACES], F32, "reuse_a")
+        z2_in = tile("z2_in", [P, PLACES, PACK], BF16)
+        nc.vector.tensor_tensor(diff[:], ea[:], ea2[:], ALU.subtract)
+        for t in range(PACK):
+            nc.vector.tensor_scalar(z2_in[:, :, t], diff[:, t, :], 3.0, gm_t[:, t : t + 1], ALU.mult, ALU.mult)
+        z2_words = tile("z2_words", [P, PLACES], U32)
+        z2_plane = tile("z2_plane", [P, PLACES], U8)
+        nc.vector.quantize_mx(out=z2_words[:].bitcast(FP8X4), scales=z2_plane[:], in_=z2_in[:].rearrange("p j t -> p (j t)"))
+
+        w2_raw = load_words("w2_raw", w2_words, "w2_raw")
+        w1_raw = load_words("w1_raw", w1_words, "w1_raw")
+        w_bytes = zeroed_bytes(nc.vector, "w_bytes", FEATURES)
+        for q in range(4):
+            rows = slice(4 * q, 4 * q + 4)
+            nc.sync.dma_start(w_bytes[32 * q : 32 * q + 4, :].bitcast(I32), w1_scales[0][rows, :].bitcast(I32))
+            nc.sync.dma_start(w_bytes[32 * q + 4 : 32 * q + 8, :].bitcast(I32), w2_scales[0][rows, :].bitcast(I32))
+        w1_dealt = tile("w1_dealt", [P, FEATURES], U32)
+        w2_dealt = tile("w2_dealt", [P, FEATURES], U32)
+        w_planes = tile("w_planes", [P, FEATURES], U8)
+        deal(w2_dealt[:], w2_raw[:])
+        deal(w1_dealt[:], w1_raw[:])
+        deal(w_planes[:], w_bytes[:])
+
+        h_banks = [ps.tile([P, PLACES], F32, name="h_bank%d" % t, tag="left%d" % t) for t in range(PACK)]
+        for t in range(PACK):
+            product(h_banks[t], w2_dealt, w_planes[4:P, :], t, z2_words[:], z2_plane[:], True, False)
+        z_words = tile("z_words", [P, PLACES], U32)
+        z_plane = tile("z_plane", [P, PLACES], U8)
+        nc.vector.quantize_mx(out=z_words[:].bitcast(FP8X4), scales=z_plane[:], in_=z_in[:].rearrange("p j t -> p (j t)"))
+        for t in range(PACK):
+            product(h_banks[t], w1_dealt, w_planes, t, z_words[:], z_plane[:], False, True)
+
+        h_rows = [tile("h_row%d" % t, [P, WIDE], F32) for t in range(PACK)]
+        sg3 = tile("sg3", [P, PACK, PLACES], F32)
+        picked = tile("picked", [P, PACK, PLACES], F32)
+        kept = tile("kept", [P, PACK, PLACES], F32)
+        result = tile("result", [P, PACK, PLACES], F32)
+        out_rows = out_0.rearrange("(p t) j -> p t j", t=PACK)
+        fetched = tile("fetched", [P, 2, PLACES], F32)
+        y_in = tile("y_in", [P, PLACES, PACK], BF16)
+        y_words = tile("y_words", [P, PLACES], U32)
+        y_plane = tile("y_plane", [P, PLACES], U8)
+        nc.scalar.copy(h_rows[0][:, 0:PLACES], h_banks[0][:])
+        for t in range(1, PACK):
+            nc.vector.tensor_copy(h_rows[t][:, 0:PLACES], h_banks[t][:])
+        for t in range(PACK):
+            col = slice(t, t + 1)
+            nc.scalar.activation(sg3[:, t, :], h_rows[t][:].indirect(n6_t[:]), ACT.Sigmoid, bias=bias_s3[:, col], scale=sl2_t[:, col])
+            if t >= 2:
+                nc.scalar.activation(fetched[:, t - 2, :], h_rows[t][:].indirect(n5_t[:]), ACT.Copy)
+            nc.vector.scalar_tensor_tensor(kept[:, t, :], sg3[:, t, :], 1.0, h_rows[t][:, 0:PLACES], ALU.subtract, ALU.mult)
+            at_n5 = fetched[:, t - 2, :] if t >= 2 else h_rows[t][:].indirect(n5_t[:])
+            nc.vector.tensor_tensor(picked[:, t, :], at_n5, sg3[:, t, :], ALU.mult)
+            nc.vector.tensor_tensor(result[:, t, :], picked[:, t, :], kept[:, t, :], ALU.subtract)
+            nc.sync.dma_start(out_rows[:, t, :], result[:, t, :])
+        nc.scalar.copy(y_in[:, :, 0:2], result[:, 0:2, :].rearrange("p t j -> p j t"))
+        nc.vector.tensor_copy(y_in[:, :, 2:4], result[:, 2:4, :].rearrange("p t j -> p j t"))
+        nc.vector.quantize_mx(out=y_words[:].bitcast(FP8X4), scales=y_plane[:], in_=y_in[:].rearrange("p j t -> p (j t)"))
+        nc.sync.dma_start(out_1[0].rearrange("p c r -> p (c r)").bitcast(I32), y_words[:].bitcast(I32))
+        for q in range(4):
+            queue = nc.scalar if q % 2 == 0 else nc.sync
+            queue.dma_start(out_2[0][4 * q : 4 * q + 4, :].bitcast(I32), y_plane[32 * q : 32 * q + 4, :].bitcast(I32))

@@ -1,6 +1,7 @@
 from contextlib import ExitStack
 
 import concourse.mybir as mybir
+from concourse.masks import make_identity
 
 F32 = mybir.dt.float32
 BF16 = mybir.dt.bfloat16
@@ -40,20 +41,25 @@ def tile_picked_pqjeodetwetr_none_po_kernel(
             nc.sync.dma_start(held[:], src)
             return held
 
-        def load_words(name, src, tag):
-            held = tile(name, [P, src.shape[2]], U32, tag)
+        def load_words(name, src):
+            held = tile(name, [P, src.shape[2]], U32)
             nc.sync.dma_start(held[:].bitcast(I32), src[0].rearrange("p c r -> p (c r)").bitcast(I32))
             return held
 
         def load_scale_table(name, src):
-            width = src.shape[2]
-            held = tile(name, [P, width], U8)
-            nc.sync.dma_start(held[:].bitcast(I32), src[0].bitcast(I32).unsqueeze(1).broadcast_to([16, 8, width // 4]))
+            held = zeroed_bytes(name, src.shape[2])
+            nc.scalar.dma_start(held[0:P:8, :].bitcast(I32), src[0].bitcast(I32))
             return held
 
-        def load_rows(name, src):
+        def load_plain_rows(queue, name, src):
             held = tile(name, [P, PACK], F32)
-            nc.gpsimd.dma_start(held[:], src.rearrange("(p t) o -> p (t o)", t=PACK))
+            with nc.allow_non_contiguous_dma(reason="one value a partition and tile"):
+                queue.dma_start(held[:], src.rearrange("(u p) o -> p (u o)", p=P))
+            return held
+
+        def load_dealt_rows(queue, name, src, tag=None):
+            held = tile(name, [P, PACK], F32, tag)
+            queue.dma_start(held[:], src.rearrange("(p t) o -> p (t o)", t=PACK))
             return held
 
         def sigmoid_bias(name, slope, threshold):
@@ -63,13 +69,13 @@ def tile_picked_pqjeodetwetr_none_po_kernel(
             nc.gpsimd.tensor_tensor(bias[:], slope[:], negated[:], ALU.mult)
             return bias
 
-        def zeroed_bytes(engine, name, width, tag=None):
-            held = tile(name, [P, width], U8, tag)
-            engine.memset(held[:].bitcast(I32), 0)
+        def zeroed_bytes(name, width):
+            held = tile(name, [P, width], U8)
+            nc.vector.memset(held[:].bitcast(I32), 0)
             return held
 
-        def deal(dst, src):
-            nc.vector.tensor_copy(dst.rearrange("p (t m) -> p m t", t=PACK), src.rearrange("p (m t) -> p m t", t=PACK))
+        def deal(dst, src, engine=nc.vector):
+            engine.tensor_copy(dst.rearrange("p (t m) -> p m t", t=PACK), src.rearrange("p (m t) -> p m t", t=PACK))
 
         def gather(dst, window, offsets):
             nc.vector.tensor_copy(dst, window[:].indirect(offsets[:]))
@@ -85,53 +91,100 @@ def tile_picked_pqjeodetwetr_none_po_kernel(
                 rhs=rhs.bitcast(FP8X4), rhs_scale=rhs_scales, start=start, stop=stop,
             )
 
-        two_t = load_list("two_t", two)
         x_bytes = load_scale_table("x_bytes", x_scales)
-        k2_t = load_list("k2_t", k2)
         d_bytes = load_scale_table("d_bytes", d_scales)
-        x_table = load_words("x_table", x_words, "x_table")
-        d_table = load_words("d_table", d_words, "d_table")
-        k1_t = load_list("k1_t", k1)
         offs_t = load_list("offs_t", offs)
-        n3_t = load_list("n3_t", n3)
-        n4_t = load_list("n4_t", n4)
-        n1_t = load_list("n1_t", n1)
+        k1_t = load_list("k1_t", k1)
         n2_t = load_list("n2_t", n2)
-        n5_t = load_list("n5_t", n5)
-        n6_t = load_list("n6_t", n6)
-        tau_t = load_rows("tau_t", tau)
-        tau2_t = load_rows("tau2_t", tau2)
-        sl_t = load_rows("sl_t", sl)
-        th_t = load_rows("th_t", th)
-        gm_t = load_rows("gm_t", gm)
-        gn_t = load_rows("gn_t", gn)
-        sl2_t = load_rows("sl2_t", sl2)
-        th2_t = load_rows("th2_t", th2)
-        bias_s = sigmoid_bias("bias_s", sl_t, th_t)
-        bias_s3 = sigmoid_bias("bias_s3", sl2_t, th2_t)
-        plane_b = zeroed_bytes(nc.vector, "plane_b", FEATURES + PLACES, "reuse_plane")
-        plane_a = zeroed_bytes(nc.vector, "plane_a", FEATURES + PLACES)
+        n1_t = load_list("n1_t", n1)
+        x_table = load_words("x_table", x_words)
+        d_table = load_words("d_table", d_words)
+        two_t = load_list("two_t", two)
+        k2_t = load_list("k2_t", k2)
+        sl_t = load_plain_rows(nc.gpsimd, "sl_t", sl)
+        th_t = load_plain_rows(nc.gpsimd, "th_t", th)
+        gn_t = load_plain_rows(nc.gpsimd, "gn_t", gn)
+        planes_a = [zeroed_bytes("plane_a0", 2 * P + PLACES), zeroed_bytes("plane_a1", 2 * P)]
+        plane_b = zeroed_bytes("plane_b", FEATURES + PLACES)
+        ident_f32 = tile("ident_f32", [P, P], F32)
+        ident_bf16 = tile("ident_bf16", [P, P], BF16)
+        make_identity(nc, ident_f32[:])
+        nc.gpsimd.tensor_copy(ident_bf16[:], ident_f32[:])
 
-        db_b = tile("db_b", [P, FEATURES], U8)
-        xb_b = tile("xb_b", [P, PLACES], U8)
+        bytes_a = [tile("bytes_a0", [P, 2 * P + PLACES], U8), tile("bytes_a1", [P, 2 * P], U8)]
+        gather(bytes_a[0][:, 2 * P :], x_bytes, offs_t)
+        for half, queue in enumerate([nc.scalar, nc.sync]):
+            gather(bytes_a[half][:, 0 : 2 * P], d_bytes, k1_t[:, 16 * half : 16 * half + 16])
+            move_scale_rows(queue, planes_a[half], bytes_a[half])
+        xw_a = tile("xw_a", [P, PLACES], U32, "reuse_x")
+        gather(xw_a[:], x_table, offs_t)
+        a_banks = [ps.tile([P, PLACES], F32, name="a_bank%d" % u, tag="wide%d" % u) for u in range(PACK)]
+        for half in range(2):
+            dw_a = tile("dw_a%d" % half, [P, 2 * P], U32, "reuse_half%d" % half)
+            gather(dw_a[:], d_table, k1_t[:, 16 * half : 16 * half + 16])
+            for i in range(2):
+                product(a_banks[2 * half + i], dw_a, planes_a[half], i, xw_a[:], planes_a[0][:, 2 * P :], True, True)
+
+        bias_s = tile("bias_s", [P, PACK], F32, "bytes_a0")
+        nc.vector.scalar_tensor_tensor(bias_s[:], sl_t[:], -1.0, th_t[:], ALU.mult, ALU.mult)
+        a_rows = [tile("a_row%d" % u, [P, PLACES], F32) for u in range(PACK)]
+        sg = tile("sg", [P, PACK, PAIRS], F32)
+        sg2 = tile("sg2", [P, PACK, PAIRS], F32)
+        pa = tile("pa", [P, PACK, PAIRS], F32)
+        pb = tile("pb", [P, PACK, PAIRS], F32)
+        ra = tile("ra", [P, PACK, PAIRS], F32)
+        rb = tile("rb", [P, PACK, PAIRS], F32)
+        for u in range(PACK):
+            col = slice(u, u + 1)
+            nc.vector.tensor_scalar(a_rows[u][:], a_banks[u][:], 0.0625, None, ALU.mult)
+            nc.scalar.activation(sg2[:, u, :], a_rows[u][:].indirect(n2_t[:]), ACT.Sigmoid, bias=bias_s[:, col], scale=sl_t[:, col])
+            nc.scalar.activation(pa[:, u, :], a_rows[u][:].indirect(n1_t[:]), ACT.Copy)
+            nc.scalar.activation(sg[:, u, :], a_rows[u][:].indirect(n1_t[:]), ACT.Sigmoid, bias=bias_s[:, col], scale=sl_t[:, col])
+            nc.scalar.activation(pb[:, u, :], a_rows[u][:].indirect(n2_t[:]), ACT.Copy)
+        for u in range(PACK):
+            nc.vector.tensor_tensor(ra[:, u, :], pa[:, u, :], sg2[:, u, :], ALU.mult)
+            nc.vector.tensor_tensor(rb[:, u, :], pb[:, u, :], sg[:, u, :], ALU.subtract)
+        dt_rows = [tile("dt_row%d" % u, [P, PLACES], F32) for u in range(PACK)]
+        nc.scalar.activation(dt_rows[0][:].indirect(n1_t[:]), ra[:, 0, :], ACT.Copy)
+        for u in range(PACK):
+            if u + 1 < PACK:
+                nc.scalar.activation(dt_rows[u + 1][:].indirect(n1_t[:]), ra[:, u + 1, :], ACT.Copy)
+            nc.scalar.activation(dt_rows[u][:].indirect(n2_t[:]), rb[:, u, :], ACT.Copy)
+
+        bytes_b = tile("bytes_b", [P, FEATURES + PLACES], U8, "reuse_half0")
         staged_b = tile("staged_b", [P, FEATURES + PLACES], U8)
-        gather(xb_b[:], x_bytes, two_t)
-        gather(db_b[:], d_bytes, k2_t)
-        nc.vector.tensor_copy(staged_b[:, FEATURES:].bitcast(I32), xb_b[:].bitcast(I32))
-        deal(staged_b[:, 0:FEATURES], db_b[:])
-        move_scale_rows(nc.scalar, plane_b, staged_b)
-        xw_b = tile("xw_b", [P, PLACES], U32, "reuse_x")
-        dw_b = tile("dw_b", [P, FEATURES], U32, "reuse_raw")
+        gather(bytes_b[:, FEATURES:], x_bytes, two_t)
+        gather(bytes_b[:, 0:FEATURES], d_bytes, k2_t)
+        nc.vector.tensor_copy(staged_b[:, FEATURES:].bitcast(I32), bytes_b[:, FEATURES:].bitcast(I32))
+        deal(staged_b[:, 0:FEATURES], bytes_b[:, 0:FEATURES])
+        move_scale_rows(nc.sync, plane_b, staged_b)
+        xw_b = tile("xw_b", [P, PLACES], U32, "reuse_half1")
+        dw_b = tile("dw_b", [P, FEATURES], U32, "reuse_x")
         dealt_b = tile("dealt_b", [P, FEATURES], U32, "reuse_dealt")
         gather(xw_b[:], x_table, two_t)
         gather(dw_b[:], d_table, k2_t)
         deal(dealt_b[:], dw_b[:])
-        b_banks = [ps.tile([P, PLACES], F32, name="b_bank%d" % t, tag="left%d" % t) for t in range(PACK)]
+        b_pairs = [ps.tile([P, 2, PLACES], F32, name="b_pair%d" % i) for i in range(2)]
         for t in range(PACK):
-            product(b_banks[t], dealt_b, plane_b, t, xw_b[:], plane_b[:, FEATURES:], True, True)
+            product(b_pairs[t // 2][:, t % 2, :], dealt_b, plane_b, t, xw_b[:], plane_b[:, FEATURES:], True, True)
 
-        db_a = tile("db_a", [P, FEATURES], U8, "reuse_raw")
-        gather(db_a[:], d_bytes, k1_t)
+        n3_t = load_list("n3_t", n3)
+        n4_t = load_list("n4_t", n4)
+        tau_t = load_dealt_rows(nc.sync, "tau_t", tau)
+        tau2_t = load_dealt_rows(nc.sync, "tau2_t", tau2)
+        w1_raw = load_words("w1_raw", w1_words)
+        w2_raw = load_words("w2_raw", w2_words)
+        gm_t = load_dealt_rows(nc.sync, "gm_t", gm)
+        n6_t = load_list("n6_t", n6)
+        n5_t = load_list("n5_t", n5)
+        sl2_t = load_dealt_rows(nc.sync, "sl2_t", sl2)
+        th2_t = load_dealt_rows(nc.sync, "th2_t", th2)
+        w_bytes = zeroed_bytes("w_bytes", FEATURES)
+        for q in range(4):
+            rows = slice(4 * q, 4 * q + 4)
+            nc.sync.dma_start(w_bytes[32 * q : 32 * q + 4, :].bitcast(I32), w1_scales[0][rows, :].bitcast(I32))
+            nc.sync.dma_start(w_bytes[32 * q + 4 : 32 * q + 8, :].bitcast(I32), w2_scales[0][rows, :].bitcast(I32))
+        bias_s3 = sigmoid_bias("bias_s3", sl2_t, th2_t)
 
         b_rows = [tile("b_row%d" % t, [P, WIDE], F32) for t in range(PACK)]
         top = tile("top", [P, PACK], F32)
@@ -139,95 +192,67 @@ def tile_picked_pqjeodetwetr_none_po_kernel(
         bias_e2 = tile("bias_e2", [P, PACK], F32)
         ea = tile("ea", [P, PACK, PLACES], F32)
         ea2 = tile("ea2", [P, PACK, PLACES], F32)
-
-        def exponentials(t):
-            col = slice(t, t + 1)
-            nc.vector.tensor_scalar(b_rows[t][:, 0:PLACES], b_banks[t][:], 0.0625, None, ALU.mult, ALU.max, accum_out=top[:, col])
-            nc.vector.tensor_scalar(bias_e[:, col], top[:, col], tau_t[:, col], -1.0, ALU.mult, ALU.mult)
-            nc.vector.tensor_scalar(bias_e2[:, col], top[:, col], tau2_t[:, col], -1.0, ALU.mult, ALU.mult)
-            nc.scalar.activation(ea[:, t, :], b_rows[t][:].indirect(n3_t[:]), ACT.Exp, bias=bias_e[:, col], scale=tau_t[:, col])
-            nc.scalar.activation(ea2[:, t, :], b_rows[t][:].indirect(n4_t[:]), ACT.Exp, bias=bias_e2[:, col], scale=tau2_t[:, col])
-
-        exponentials(0)
-        exponentials(1)
-        xb_a = tile("xb_a", [P, PLACES], U8, "reuse_x")
-        staged_a = tile("staged_a", [P, FEATURES + PLACES], U8)
-        gather(xb_a[:], x_bytes, offs_t)
-        deal(staged_a[:, 0:FEATURES], db_a[:])
-        nc.vector.tensor_copy(staged_a[:, FEATURES:].bitcast(I32), xb_a[:].bitcast(I32))
-        move_scale_rows(nc.sync, plane_a, staged_a)
-        exponentials(2)
-        exponentials(3)
-
-        xw_a = tile("xw_a", [P, PLACES], U32, "reuse_plane")
-        dw_a = tile("dw_a", [P, FEATURES], U32, "reuse_dealt")
-        dealt_a = tile("dealt_a", [P, FEATURES], U32, "reuse_a")
-        gather(xw_a[:], x_table, offs_t)
-        gather(dw_a[:], d_table, k1_t)
-        deal(dealt_a[:], dw_a[:])
-        a_banks = [ps.tile([P, PLACES], F32, name="a_bank%d" % t, tag="right%d" % t) for t in range(PACK)]
         for t in range(PACK):
-            product(a_banks[t], dealt_a, plane_a, t, xw_a[:], plane_a[:, FEATURES:], True, True)
+            nc.vector.tensor_scalar(
+                b_rows[t][:, 0:PLACES], b_pairs[t // 2][:, t % 2, :], 0.0625, None, ALU.mult, ALU.max, accum_out=top[:, t : t + 1]
+            )
+        nc.vector.scalar_tensor_tensor(bias_e[:], top[:], -1.0, tau_t[:], ALU.mult, ALU.mult)
+        nc.vector.scalar_tensor_tensor(bias_e2[:], top[:], -1.0, tau2_t[:], ALU.mult, ALU.mult)
 
+        z_plain = tile("z_plain", [P, PACK, PLACES], BF16, "reuse_dealt")
+        turned = ps.tile([P, 2, FEATURES], BF16, name="turned")
+        for u in range(PACK):
+            nc.vector.tensor_scalar(z_plain[:, u, :], dt_rows[u][:], gn_t[:, u : u + 1], None, ALU.mult)
+            for c in range(2):
+                nc.tensor.transpose(turned[:, c, P * u : P * (u + 1)], z_plain[:, u, P * c : P * (c + 1)], ident_bf16[:])
+        z_pairs = tile("z_pairs", [P, 2, 2, P], F32)
+        nc.vector.tensor_copy(
+            z_pairs[:], turned[:].rearrange("p c r -> p (c r)").bitcast(F32).rearrange("p (c m e) -> p c e m", c=2, e=2)
+        )
+        back = ps.tile([P, 2, 2, P], F32, name="back")
+        for c in range(2):
+            for e in range(2):
+                nc.tensor.transpose(back[:, c, e, :], z_pairs[:, c, e, :], ident_f32[:])
+        z_in = tile("z_in", [P, PLACES * PACK], BF16)
+        nc.vector.tensor_copy(
+            z_in[:].bitcast(F32).rearrange("p (c j e) -> p c j e", c=2, e=2), back[:].rearrange("p c e j -> p c j e")
+        )
+        z_words = tile("z_words", [P, PLACES], U32)
+        z_plane = tile("z_plane", [P, PLACES], U8)
+        nc.vector.quantize_mx(out=z_words[:].bitcast(FP8X4), scales=z_plane[:], in_=z_in[:])
 
-        a_rows = [tile("a_row%d" % t, [P, PLACES], F32) for t in range(PACK)]
-        sg = tile("sg", [P, PACK, PAIRS], F32)
-        sg2 = tile("sg2", [P, PACK, PAIRS], F32)
-        pa = tile("pa", [P, PACK, PAIRS], F32)
-        pb = tile("pb", [P, PACK, PAIRS], F32)
-        ra = tile("ra", [P, PACK, PAIRS], F32)
-        rb = tile("rb", [P, PACK, PAIRS], F32)
-        for t in range(PACK):
-            col = slice(t, t + 1)
-            nc.vector.tensor_scalar(a_rows[t][:], a_banks[t][:], 0.0625, None, ALU.mult)
-            nc.scalar.activation(sg2[:, t, :], a_rows[t][:].indirect(n2_t[:]), ACT.Sigmoid, bias=bias_s[:, col], scale=sl_t[:, col])
-            nc.scalar.activation(pa[:, t, :], a_rows[t][:].indirect(n1_t[:]), ACT.Copy)
-            nc.scalar.activation(sg[:, t, :], a_rows[t][:].indirect(n1_t[:]), ACT.Sigmoid, bias=bias_s[:, col], scale=sl_t[:, col])
-            nc.scalar.activation(pb[:, t, :], a_rows[t][:].indirect(n2_t[:]), ACT.Copy)
-        for t in range(PACK):
-            nc.vector.tensor_tensor(ra[:, t, :], pa[:, t, :], sg2[:, t, :], ALU.mult)
-            nc.vector.tensor_tensor(rb[:, t, :], pb[:, t, :], sg[:, t, :], ALU.subtract)
-
-        dt_rows = [tile("dt_row%d" % t, [P, PLACES], F32) for t in range(PACK)]
-        z_in = tile("z_in", [P, PLACES, PACK], BF16)
-        nc.scalar.activation(dt_rows[0][:].indirect(n1_t[:]), ra[:, 0, :], ACT.Copy)
-        for t in range(PACK):
-            if t + 1 < PACK:
-                nc.scalar.activation(dt_rows[t + 1][:].indirect(n1_t[:]), ra[:, t + 1, :], ACT.Copy)
-            nc.scalar.activation(dt_rows[t][:].indirect(n2_t[:]), rb[:, t, :], ACT.Copy)
-            nc.vector.tensor_scalar(z_in[:, :, t], dt_rows[t][:], gn_t[:, t : t + 1], None, ALU.mult)
-
-        diff = tile("diff", [P, PACK, PLACES], F32, "reuse_a")
-        z2_in = tile("z2_in", [P, PLACES, PACK], BF16)
-        nc.vector.tensor_tensor(diff[:], ea[:], ea2[:], ALU.subtract)
-        for t in range(PACK):
-            nc.vector.tensor_scalar(z2_in[:, :, t], diff[:, t, :], 3.0, gm_t[:, t : t + 1], ALU.mult, ALU.mult)
-        z2_words = tile("z2_words", [P, PLACES], U32)
-        z2_plane = tile("z2_plane", [P, PLACES], U8)
-        nc.vector.quantize_mx(out=z2_words[:].bitcast(FP8X4), scales=z2_plane[:], in_=z2_in[:].rearrange("p j t -> p (j t)"))
-
-        w2_raw = load_words("w2_raw", w2_words, "w2_raw")
-        w1_raw = load_words("w1_raw", w1_words, "w1_raw")
-        w_bytes = zeroed_bytes(nc.vector, "w_bytes", FEATURES)
-        for q in range(4):
-            rows = slice(4 * q, 4 * q + 4)
-            nc.sync.dma_start(w_bytes[32 * q : 32 * q + 4, :].bitcast(I32), w1_scales[0][rows, :].bitcast(I32))
-            nc.sync.dma_start(w_bytes[32 * q + 4 : 32 * q + 8, :].bitcast(I32), w2_scales[0][rows, :].bitcast(I32))
         w1_dealt = tile("w1_dealt", [P, FEATURES], U32)
         w2_dealt = tile("w2_dealt", [P, FEATURES], U32)
         w_planes = tile("w_planes", [P, FEATURES], U8)
-        deal(w2_dealt[:], w2_raw[:])
+        deal(w_planes[:], w_bytes[:], nc.gpsimd)
         deal(w1_dealt[:], w1_raw[:])
-        deal(w_planes[:], w_bytes[:])
+        deal(w2_dealt[:], w2_raw[:])
+        h_banks = [ps.tile([P, PLACES], F32, name="h_bank%d" % t, tag="wide%d" % t) for t in range(PACK)]
+        for t in range(PACK):
+            product(h_banks[t], w1_dealt, w_planes, t, z_words[:], z_plane[:], True, False)
 
-        h_banks = [ps.tile([P, PLACES], F32, name="h_bank%d" % t, tag="left%d" % t) for t in range(PACK)]
-        for t in range(PACK):
-            product(h_banks[t], w2_dealt, w_planes[4:P, :], t, z2_words[:], z2_plane[:], True, False)
-        z_words = tile("z_words", [P, PLACES], U32)
-        z_plane = tile("z_plane", [P, PLACES], U8)
-        nc.vector.quantize_mx(out=z_words[:].bitcast(FP8X4), scales=z_plane[:], in_=z_in[:].rearrange("p j t -> p (j t)"))
-        for t in range(PACK):
-            product(h_banks[t], w1_dealt, w_planes, t, z_words[:], z_plane[:], False, True)
+        diff = tile("diff", [P, PACK, PLACES], F32)
+        z2_in = tile("z2_in", [P, PLACES, PACK], BF16)
+        z2_words = tile("z2_words", [P, PLACES], U32)
+        z2_plane = tile("z2_plane", [P, PLACES], U8)
+
+        def difference(t, lo, hi):
+            col, cols, entries = slice(t, t + 1), slice(lo, hi), slice(lo // 16, hi // 16)
+            nc.scalar.activation(ea[:, t, cols], b_rows[t][:].indirect(n3_t[:, entries]), ACT.Exp, bias=bias_e[:, col], scale=tau_t[:, col])
+            nc.scalar.activation(ea2[:, t, cols], b_rows[t][:].indirect(n4_t[:, entries]), ACT.Exp, bias=bias_e2[:, col], scale=tau2_t[:, col])
+            nc.vector.tensor_tensor(diff[:, t, cols], ea[:, t, cols], ea2[:, t, cols], ALU.subtract)
+            nc.vector.tensor_scalar(z2_in[:, cols, t], diff[:, t, cols], 3.0, gm_t[:, col], ALU.mult, ALU.mult)
+
+        for t in range(PACK - 1):
+            difference(t, 0, PLACES)
+        for half in range(2):
+            cols = slice(P * half, P * (half + 1))
+            difference(PACK - 1, cols.start, cols.stop)
+            nc.vector.quantize_mx(
+                out=z2_words[:, cols].bitcast(FP8X4), scales=z2_plane[:, cols], in_=z2_in[:, cols, :].rearrange("p j t -> p (j t)")
+            )
+            for t in range(PACK):
+                product(h_banks[t][:, cols], w2_dealt, w_planes[4:P, :], t, z2_words[:, cols], z2_plane[:, cols], False, half == 1)
 
         h_rows = [tile("h_row%d" % t, [P, WIDE], F32) for t in range(PACK)]
         sg3 = tile("sg3", [P, PACK, PLACES], F32)
@@ -239,8 +264,7 @@ def tile_picked_pqjeodetwetr_none_po_kernel(
         y_in = tile("y_in", [P, PLACES, PACK], BF16)
         y_words = tile("y_words", [P, PLACES], U32)
         y_plane = tile("y_plane", [P, PLACES], U8)
-        nc.scalar.copy(h_rows[0][:, 0:PLACES], h_banks[0][:])
-        for t in range(1, PACK):
+        for t in range(PACK):
             nc.vector.tensor_copy(h_rows[t][:, 0:PLACES], h_banks[t][:])
         for t in range(PACK):
             col = slice(t, t + 1)

@@ -51,10 +51,10 @@ def tile_picked_pqjeodetwetr_none_po_kernel(
             nc.scalar.dma_start(held[0:P:8, :].bitcast(I32), src[0].bitcast(I32))
             return held
 
-        def load_plain_rows(queue, name, src):
-            held = tile(name, [P, PACK], F32)
+        def load_plain_rows(name, src, tag=None):
+            held = tile(name, [P, PACK], F32, tag)
             with nc.allow_non_contiguous_dma(reason="one value a partition and tile"):
-                queue.dma_start(held[:], src.rearrange("(u p) o -> p (u o)", p=P))
+                nc.gpsimd.dma_start(held[:], src.rearrange("(u p) o -> p (u o)", p=P))
             return held
 
         def load_dealt_rows(queue, name, src, tag=None):
@@ -101,9 +101,8 @@ def tile_picked_pqjeodetwetr_none_po_kernel(
         d_table = load_words("d_table", d_words)
         two_t = load_list("two_t", two)
         k2_t = load_list("k2_t", k2)
-        sl_t = load_plain_rows(nc.gpsimd, "sl_t", sl)
-        th_t = load_plain_rows(nc.gpsimd, "th_t", th)
-        gn_t = load_plain_rows(nc.gpsimd, "gn_t", gn)
+        sl_t = load_plain_rows("sl_t", sl)
+        th_t = load_plain_rows("th_t", th)
         planes_a = [zeroed_bytes("plane_a0", 2 * P + PLACES), zeroed_bytes("plane_a1", 2 * P)]
         plane_b = zeroed_bytes("plane_b", FEATURES + PLACES)
         ident_f32 = tile("ident_f32", [P, P], F32)
@@ -127,6 +126,7 @@ def tile_picked_pqjeodetwetr_none_po_kernel(
 
         bias_s = tile("bias_s", [P, PACK], F32, "bytes_a0")
         nc.vector.scalar_tensor_tensor(bias_s[:], sl_t[:], -1.0, th_t[:], ALU.mult, ALU.mult)
+        gn_t = load_plain_rows("gn_t", gn, "bytes_a1")
         a_rows = [tile("a_row%d" % u, [P, PLACES], F32) for u in range(PACK)]
         sg = tile("sg", [P, PACK, PAIRS], F32)
         sg2 = tile("sg2", [P, PACK, PAIRS], F32)
@@ -164,7 +164,7 @@ def tile_picked_pqjeodetwetr_none_po_kernel(
         gather(xw_b[:], x_table, two_t)
         gather(dw_b[:], d_table, k2_t)
         deal(dealt_b[:], dw_b[:])
-        b_pairs = [ps.tile([P, 2, PLACES], F32, name="b_pair%d" % i) for i in range(2)]
+        b_pairs = [ps.tile([P, 2, PLACES], F32, name="b_pair%d" % i, tag="b_pair%d" % i) for i in range(2)]
         for t in range(PACK):
             product(b_pairs[t // 2][:, t % 2, :], dealt_b, plane_b, t, xw_b[:], plane_b[:, FEATURES:], True, True)
 
@@ -200,7 +200,7 @@ def tile_picked_pqjeodetwetr_none_po_kernel(
         nc.vector.scalar_tensor_tensor(bias_e2[:], top[:], -1.0, tau2_t[:], ALU.mult, ALU.mult)
 
         z_plain = tile("z_plain", [P, PACK, PLACES], BF16, "reuse_dealt")
-        turned = ps.tile([P, 2, FEATURES], BF16, name="turned")
+        turned = ps.tile([P, 2, FEATURES], BF16, name="turned", tag="turned")
         for u in range(PACK):
             nc.vector.tensor_scalar(z_plain[:, u, :], dt_rows[u][:], gn_t[:, u : u + 1], None, ALU.mult)
             for c in range(2):
@@ -209,7 +209,7 @@ def tile_picked_pqjeodetwetr_none_po_kernel(
         nc.vector.tensor_copy(
             z_pairs[:], turned[:].rearrange("p c r -> p (c r)").bitcast(F32).rearrange("p (c m e) -> p c e m", c=2, e=2)
         )
-        back = ps.tile([P, 2, 2, P], F32, name="back")
+        back = ps.tile([P, 2, 2, P], F32, name="back", tag="back")
         for c in range(2):
             for e in range(2):
                 nc.tensor.transpose(back[:, c, e, :], z_pairs[:, c, e, :], ident_f32[:])
@@ -227,9 +227,13 @@ def tile_picked_pqjeodetwetr_none_po_kernel(
         deal(w_planes[:], w_bytes[:], nc.gpsimd)
         deal(w1_dealt[:], w1_raw[:])
         deal(w2_dealt[:], w2_raw[:])
-        h_banks = [ps.tile([P, PLACES], F32, name="h_bank%d" % t, tag="wide%d" % t) for t in range(PACK)]
-        for t in range(PACK):
-            product(h_banks[t], w1_dealt, w_planes, t, z_words[:], z_plane[:], True, False)
+        halves = [slice(0, P), slice(P, PLACES)]
+        free_banks = [["b_pair0", "b_pair1", "turned", "back"], ["wide%d" % t for t in range(PACK)]]
+        h_banks = [[ps.tile([P, P], F32, name="h_bank%d%d" % (half, t), tag=free_banks[half][t]) for t in range(PACK)] for half in range(2)]
+        for half, cols in enumerate(halves):
+            for t in range(PACK):
+                product(h_banks[half][t], w1_dealt, w_planes, t, z_words[:, cols], z_plane[:, cols], True, False)
+        h_rows = [tile("h_row%d" % t, [P, WIDE], F32) for t in range(PACK)]
 
         diff = tile("diff", [P, PACK, PLACES], F32)
         z2_in = tile("z2_in", [P, PLACES, PACK], BF16)
@@ -243,18 +247,20 @@ def tile_picked_pqjeodetwetr_none_po_kernel(
             nc.vector.tensor_tensor(diff[:, t, cols], ea[:, t, cols], ea2[:, t, cols], ALU.subtract)
             nc.vector.tensor_scalar(z2_in[:, cols, t], diff[:, t, cols], 3.0, gm_t[:, col], ALU.mult, ALU.mult)
 
-        for t in range(PACK - 1):
+        for t in range(2):
             difference(t, 0, PLACES)
-        for half in range(2):
-            cols = slice(P * half, P * (half + 1))
-            difference(PACK - 1, cols.start, cols.stop)
+        for half, cols in enumerate(halves):
+            for t in range(2, PACK):
+                difference(t, cols.start, cols.stop)
             nc.vector.quantize_mx(
                 out=z2_words[:, cols].bitcast(FP8X4), scales=z2_plane[:, cols], in_=z2_in[:, cols, :].rearrange("p j t -> p (j t)")
             )
             for t in range(PACK):
-                product(h_banks[t][:, cols], w2_dealt, w_planes[4:P, :], t, z2_words[:, cols], z2_plane[:, cols], False, half == 1)
+                product(h_banks[half][t], w2_dealt, w_planes[4:P, :], t, z2_words[:, cols], z2_plane[:, cols], False, True)
+        for t in range(PACK):
+            for half, cols in enumerate(halves):
+                nc.vector.tensor_copy(h_rows[t][:, cols], h_banks[half][t][:])
 
-        h_rows = [tile("h_row%d" % t, [P, WIDE], F32) for t in range(PACK)]
         sg3 = tile("sg3", [P, PACK, PLACES], F32)
         picked = tile("picked", [P, PACK, PLACES], F32)
         kept = tile("kept", [P, PACK, PLACES], F32)
@@ -264,21 +270,29 @@ def tile_picked_pqjeodetwetr_none_po_kernel(
         y_in = tile("y_in", [P, PLACES, PACK], BF16)
         y_words = tile("y_words", [P, PLACES], U32)
         y_plane = tile("y_plane", [P, PLACES], U8)
-        for t in range(PACK):
-            nc.vector.tensor_copy(h_rows[t][:, 0:PLACES], h_banks[t][:])
+        whole = [slice(0, PLACES)]
         for t in range(PACK):
             col = slice(t, t + 1)
-            nc.scalar.activation(sg3[:, t, :], h_rows[t][:].indirect(n6_t[:]), ACT.Sigmoid, bias=bias_s3[:, col], scale=sl2_t[:, col])
-            if t >= 2:
-                nc.scalar.activation(fetched[:, t - 2, :], h_rows[t][:].indirect(n5_t[:]), ACT.Copy)
-            nc.vector.scalar_tensor_tensor(kept[:, t, :], sg3[:, t, :], 1.0, h_rows[t][:, 0:PLACES], ALU.subtract, ALU.mult)
-            at_n5 = fetched[:, t - 2, :] if t >= 2 else h_rows[t][:].indirect(n5_t[:])
-            nc.vector.tensor_tensor(picked[:, t, :], at_n5, sg3[:, t, :], ALU.mult)
-            nc.vector.tensor_tensor(result[:, t, :], picked[:, t, :], kept[:, t, :], ALU.subtract)
+            for cols in halves if t == 0 else whole:
+                entries = slice(cols.start // 16, cols.stop // 16)
+                nc.scalar.activation(
+                    sg3[:, t, cols], h_rows[t][:].indirect(n6_t[:, entries]), ACT.Sigmoid, bias=bias_s3[:, col], scale=sl2_t[:, col]
+                )
+                if t >= 2:
+                    nc.scalar.activation(fetched[:, t - 2, :], h_rows[t][:].indirect(n5_t[:]), ACT.Copy)
+                nc.vector.scalar_tensor_tensor(kept[:, t, cols], sg3[:, t, cols], 1.0, h_rows[t][:, cols], ALU.subtract, ALU.mult)
+                at_n5 = fetched[:, t - 2, :] if t >= 2 else h_rows[t][:].indirect(n5_t[:, entries])
+                nc.vector.tensor_tensor(picked[:, t, cols], at_n5, sg3[:, t, cols], ALU.mult)
+            for cols in halves if t == PACK - 1 else whole:
+                nc.vector.tensor_tensor(result[:, t, cols], picked[:, t, cols], kept[:, t, cols], ALU.subtract)
             nc.sync.dma_start(out_rows[:, t, :], result[:, t, :])
         nc.scalar.copy(y_in[:, :, 0:2], result[:, 0:2, :].rearrange("p t j -> p j t"))
-        nc.vector.tensor_copy(y_in[:, :, 2:4], result[:, 2:4, :].rearrange("p t j -> p j t"))
-        nc.vector.quantize_mx(out=y_words[:].bitcast(FP8X4), scales=y_plane[:], in_=y_in[:].rearrange("p j t -> p (j t)"))
+        for cols in halves:
+            nc.vector.tensor_copy(y_in[:, cols, 2:4], result[:, 2:4, cols].rearrange("p t j -> p j t"))
+        for cols in halves:
+            nc.vector.quantize_mx(
+                out=y_words[:, cols].bitcast(FP8X4), scales=y_plane[:, cols], in_=y_in[:, cols, :].rearrange("p j t -> p (j t)")
+            )
         nc.sync.dma_start(out_1[0].rearrange("p c r -> p (c r)").bitcast(I32), y_words[:].bitcast(I32))
         for q in range(4):
             queue = nc.scalar if q % 2 == 0 else nc.sync

from contextlib import ExitStack

import concourse.mybir as mybir
from concourse.masks import make_identity

F32 = mybir.dt.float32
BF16 = mybir.dt.bfloat16
I32 = mybir.dt.int32
U32 = mybir.dt.uint32
U16 = mybir.dt.uint16
U8 = mybir.dt.uint8
FP8X4 = mybir.dt.float8_e4m3fn_x4
ALU = mybir.AluOpType
ACT = mybir.ActivationFunctionType

P = 128
PACK = 4
TOKENS = 1024
CODEWORDS = 2048
FEATURES = 512
PLACES = 256
PAIRS = 128
WIDE = 2 * PLACES
FLOPS = 4 * 2 * 512 * 512 * 256


def tile_picked_pqjeodetwetr_none_po_kernel(
    tc, x_words, x_scales, d_words, d_scales, sl, th, tau, tau2, gn, gm, w1_words, w1_scales, w2_words, w2_scales,
    sl2, th2, offs, k1, two, k2, n1, n2, n3, n4, n5, n6, out_0, out_1, out_2,
):
    nc = tc.nc
    with ExitStack() as ctx:
        sb = ctx.enter_context(tc.tile_pool(name="sb", bufs=1))
        ps = ctx.enter_context(tc.psum_pool(name="ps", bufs=1))

        def tile(name, shape, dtype, tag=None):
            return sb.tile(shape, dtype, name=name, tag=tag or name, align_bytes=64)

        def load_list(name, src):
            held = tile(name, list(src.shape), U16)
            nc.sync.dma_start(held[:], src)
            return held

        def load_words(name, src):
            held = tile(name, [P, src.shape[2]], U32)
            nc.sync.dma_start(held[:].bitcast(I32), src[0].rearrange("p c r -> p (c r)").bitcast(I32))
            return held

        def load_scale_table(name, src):
            held = zeroed_bytes(name, src.shape[2])
            nc.scalar.dma_start(held[0:P:8, :].bitcast(I32), src[0].bitcast(I32))
            return held

        def load_plain_rows(name, src, tag=None):
            held = tile(name, [P, PACK], F32, tag)
            with nc.allow_non_contiguous_dma(reason="one value a partition and tile"):
                nc.gpsimd.dma_start(held[:], src.rearrange("(u p) o -> p (u o)", p=P))
            return held

        def load_dealt_rows(queue, name, src, tag=None):
            held = tile(name, [P, PACK], F32, tag)
            queue.dma_start(held[:], src.rearrange("(p t) o -> p (t o)", t=PACK))
            return held

        def sigmoid_bias(name, slope, threshold):
            negated = tile(name + "_neg", [P, PACK], F32)
            bias = tile(name, [P, PACK], F32)
            nc.gpsimd.tensor_scalar(negated[:], threshold[:], -1.0, 0.0, ALU.mult, ALU.add)
            nc.gpsimd.tensor_tensor(bias[:], slope[:], negated[:], ALU.mult)
            return bias

        def zeroed_bytes(name, width):
            held = tile(name, [P, width], U8)
            nc.vector.memset(held[:].bitcast(I32), 0)
            return held

        def deal(dst, src, engine=nc.vector):
            engine.tensor_copy(dst.rearrange("p (t m) -> p m t", t=PACK), src.rearrange("p (m t) -> p m t", t=PACK))

        def gather(dst, window, offsets):
            nc.vector.tensor_copy(dst, window[:].indirect(offsets[:]))

        def move_scale_rows(queue, plane, staged):
            for r in range(4):
                queue.dma_start(plane[r:P:32, :].bitcast(I32), staged[8 * r : P : 32, :].bitcast(I32))

        def product(bank, words, scales, t, rhs, rhs_scales, start, stop):
            cols = slice(P * t, P * (t + 1))
            nc.tensor.matmul_mx(
                out=bank[:], lhsT=words[:, cols].bitcast(FP8X4), lhsT_scale=scales[:, cols],
                rhs=rhs.bitcast(FP8X4), rhs_scale=rhs_scales, start=start, stop=stop,
            )

        x_bytes = load_scale_table("x_bytes", x_scales)
        d_bytes = load_scale_table("d_bytes", d_scales)
        offs_t = load_list("offs_t", offs)
        k1_t = load_list("k1_t", k1)
        n2_t = load_list("n2_t", n2)
        n1_t = load_list("n1_t", n1)
        x_table = load_words("x_table", x_words)
        d_table = load_words("d_table", d_words)
        two_t = load_list("two_t", two)
        k2_t = load_list("k2_t", k2)
        sl_t = load_plain_rows("sl_t", sl)
        th_t = load_plain_rows("th_t", th)
        planes_a = [zeroed_bytes("plane_a0", 2 * P + PLACES), zeroed_bytes("plane_a1", 2 * P)]
        plane_b = zeroed_bytes("plane_b", FEATURES + PLACES)
        ident_f32 = tile("ident_f32", [P, P], F32)
        ident_bf16 = tile("ident_bf16", [P, P], BF16)
        make_identity(nc, ident_f32[:])
        nc.gpsimd.tensor_copy(ident_bf16[:], ident_f32[:])

        bytes_a = [tile("bytes_a0", [P, 2 * P + PLACES], U8), tile("bytes_a1", [P, 2 * P], U8)]
        gather(bytes_a[0][:, 2 * P :], x_bytes, offs_t)
        for half, queue in enumerate([nc.scalar, nc.sync]):
            gather(bytes_a[half][:, 0 : 2 * P], d_bytes, k1_t[:, 16 * half : 16 * half + 16])
            move_scale_rows(queue, planes_a[half], bytes_a[half])
        xw_a = tile("xw_a", [P, PLACES], U32, "reuse_x")
        gather(xw_a[:], x_table, offs_t)
        a_banks = [ps.tile([P, PLACES], F32, name="a_bank%d" % u, tag="wide%d" % u) for u in range(PACK)]
        for half in range(2):
            dw_a = tile("dw_a%d" % half, [P, 2 * P], U32, "reuse_half%d" % half)
            gather(dw_a[:], d_table, k1_t[:, 16 * half : 16 * half + 16])
            for i in range(2):
                product(a_banks[2 * half + i], dw_a, planes_a[half], i, xw_a[:], planes_a[0][:, 2 * P :], True, True)

        bias_s = tile("bias_s", [P, PACK], F32, "bytes_a0")
        nc.vector.scalar_tensor_tensor(bias_s[:], sl_t[:], -1.0, th_t[:], ALU.mult, ALU.mult)
        gn_t = load_plain_rows("gn_t", gn, "bytes_a1")
        a_rows = [tile("a_row%d" % u, [P, PLACES], F32) for u in range(PACK)]
        sg = tile("sg", [P, PACK, PAIRS], F32)
        sg2 = tile("sg2", [P, PACK, PAIRS], F32)
        pa = tile("pa", [P, PACK, PAIRS], F32)
        pb = tile("pb", [P, PACK, PAIRS], F32)
        ra = tile("ra", [P, PACK, PAIRS], F32)
        rb = tile("rb", [P, PACK, PAIRS], F32)
        for u in range(PACK):
            col = slice(u, u + 1)
            nc.vector.tensor_scalar(a_rows[u][:], a_banks[u][:], 0.0625, None, ALU.mult)
            nc.scalar.activation(sg2[:, u, :], a_rows[u][:].indirect(n2_t[:]), ACT.Sigmoid, bias=bias_s[:, col], scale=sl_t[:, col])
            nc.scalar.activation(pa[:, u, :], a_rows[u][:].indirect(n1_t[:]), ACT.Copy)
            nc.scalar.activation(sg[:, u, :], a_rows[u][:].indirect(n1_t[:]), ACT.Sigmoid, bias=bias_s[:, col], scale=sl_t[:, col])
            nc.scalar.activation(pb[:, u, :], a_rows[u][:].indirect(n2_t[:]), ACT.Copy)
        for u in range(PACK):
            nc.vector.tensor_tensor(ra[:, u, :], pa[:, u, :], sg2[:, u, :], ALU.mult)
            nc.vector.tensor_tensor(rb[:, u, :], pb[:, u, :], sg[:, u, :], ALU.subtract)
        dt_rows = [tile("dt_row%d" % u, [P, PLACES], F32) for u in range(PACK)]
        nc.scalar.activation(dt_rows[0][:].indirect(n1_t[:]), ra[:, 0, :], ACT.Copy)
        for u in range(PACK):
            if u + 1 < PACK:
                nc.scalar.activation(dt_rows[u + 1][:].indirect(n1_t[:]), ra[:, u + 1, :], ACT.Copy)
            nc.scalar.activation(dt_rows[u][:].indirect(n2_t[:]), rb[:, u, :], ACT.Copy)

        bytes_b = tile("bytes_b", [P, FEATURES + PLACES], U8, "reuse_half0")
        staged_b = tile("staged_b", [P, FEATURES + PLACES], U8)
        gather(bytes_b[:, FEATURES:], x_bytes, two_t)
        gather(bytes_b[:, 0:FEATURES], d_bytes, k2_t)
        nc.vector.tensor_copy(staged_b[:, FEATURES:].bitcast(I32), bytes_b[:, FEATURES:].bitcast(I32))
        deal(staged_b[:, 0:FEATURES], bytes_b[:, 0:FEATURES])
        move_scale_rows(nc.sync, plane_b, staged_b)
        xw_b = tile("xw_b", [P, PLACES], U32, "reuse_half1")
        dw_b = tile("dw_b", [P, FEATURES], U32, "reuse_x")
        dealt_b = tile("dealt_b", [P, FEATURES], U32, "reuse_dealt")
        gather(xw_b[:], x_table, two_t)
        gather(dw_b[:], d_table, k2_t)
        deal(dealt_b[:], dw_b[:])
        b_pairs = [ps.tile([P, 2, PLACES], F32, name="b_pair%d" % i, tag="b_pair%d" % i) for i in range(2)]
        for t in range(PACK):
            product(b_pairs[t // 2][:, t % 2, :], dealt_b, plane_b, t, xw_b[:], plane_b[:, FEATURES:], True, True)

        n3_t = load_list("n3_t", n3)
        n4_t = load_list("n4_t", n4)
        tau_t = load_dealt_rows(nc.sync, "tau_t", tau)
        tau2_t = load_dealt_rows(nc.sync, "tau2_t", tau2)
        w1_raw = load_words("w1_raw", w1_words)
        w2_raw = load_words("w2_raw", w2_words)
        gm_t = load_dealt_rows(nc.sync, "gm_t", gm)
        n6_t = load_list("n6_t", n6)
        n5_t = load_list("n5_t", n5)
        sl2_t = load_dealt_rows(nc.sync, "sl2_t", sl2)
        th2_t = load_dealt_rows(nc.sync, "th2_t", th2)
        w_bytes = zeroed_bytes("w_bytes", FEATURES)
        for q in range(4):
            rows = slice(4 * q, 4 * q + 4)
            nc.sync.dma_start(w_bytes[32 * q : 32 * q + 4, :].bitcast(I32), w1_scales[0][rows, :].bitcast(I32))
            nc.sync.dma_start(w_bytes[32 * q + 4 : 32 * q + 8, :].bitcast(I32), w2_scales[0][rows, :].bitcast(I32))
        bias_s3 = sigmoid_bias("bias_s3", sl2_t, th2_t)

        b_rows = [tile("b_row%d" % t, [P, WIDE], F32) for t in range(PACK)]
        top = tile("top", [P, PACK], F32)
        bias_e = tile("bias_e", [P, PACK], F32)
        bias_e2 = tile("bias_e2", [P, PACK], F32)
        ea = tile("ea", [P, PACK, PLACES], F32)
        ea2 = tile("ea2", [P, PACK, PLACES], F32)
        for t in range(PACK):
            nc.vector.tensor_scalar(
                b_rows[t][:, 0:PLACES], b_pairs[t // 2][:, t % 2, :], 0.0625, None, ALU.mult, ALU.max, accum_out=top[:, t : t + 1]
            )
        nc.vector.scalar_tensor_tensor(bias_e[:], top[:], -1.0, tau_t[:], ALU.mult, ALU.mult)
        nc.vector.scalar_tensor_tensor(bias_e2[:], top[:], -1.0, tau2_t[:], ALU.mult, ALU.mult)

        z_plain = tile("z_plain", [P, PACK, PLACES], BF16, "reuse_dealt")
        turned = ps.tile([P, 2, FEATURES], BF16, name="turned", tag="turned")
        for u in range(PACK):
            nc.vector.tensor_scalar(z_plain[:, u, :], dt_rows[u][:], gn_t[:, u : u + 1], None, ALU.mult)
            for c in range(2):
                nc.tensor.transpose(turned[:, c, P * u : P * (u + 1)], z_plain[:, u, P * c : P * (c + 1)], ident_bf16[:])
        z_pairs = tile("z_pairs", [P, 2, 2, P], F32)
        nc.vector.tensor_copy(
            z_pairs[:], turned[:].rearrange("p c r -> p (c r)").bitcast(F32).rearrange("p (c m e) -> p c e m", c=2, e=2)
        )
        back = ps.tile([P, 2, 2, P], F32, name="back", tag="back")
        for c in range(2):
            for e in range(2):
                nc.tensor.transpose(back[:, c, e, :], z_pairs[:, c, e, :], ident_f32[:])
        z_in = tile("z_in", [P, PLACES * PACK], BF16)
        nc.vector.tensor_copy(
            z_in[:].bitcast(F32).rearrange("p (c j e) -> p c j e", c=2, e=2), back[:].rearrange("p c e j -> p c j e")
        )
        z_words = tile("z_words", [P, PLACES], U32)
        z_plane = tile("z_plane", [P, PLACES], U8)
        nc.vector.quantize_mx(out=z_words[:].bitcast(FP8X4), scales=z_plane[:], in_=z_in[:])

        w1_dealt = tile("w1_dealt", [P, FEATURES], U32)
        w2_dealt = tile("w2_dealt", [P, FEATURES], U32)
        w_planes = tile("w_planes", [P, FEATURES], U8)
        deal(w_planes[:], w_bytes[:], nc.gpsimd)
        deal(w1_dealt[:], w1_raw[:])
        deal(w2_dealt[:], w2_raw[:])
        halves = [slice(0, P), slice(P, PLACES)]
        free_banks = [["b_pair0", "b_pair1", "turned", "back"], ["wide%d" % t for t in range(PACK)]]
        h_banks = [[ps.tile([P, P], F32, name="h_bank%d%d" % (half, t), tag=free_banks[half][t]) for t in range(PACK)] for half in range(2)]
        for half, cols in enumerate(halves):
            for t in range(PACK):
                product(h_banks[half][t], w1_dealt, w_planes, t, z_words[:, cols], z_plane[:, cols], True, False)
        h_rows = [tile("h_row%d" % t, [P, WIDE], F32) for t in range(PACK)]

        diff = tile("diff", [P, PACK, PLACES], F32)
        z2_in = tile("z2_in", [P, PLACES, PACK], BF16)
        z2_words = tile("z2_words", [P, PLACES], U32)
        z2_plane = tile("z2_plane", [P, PLACES], U8)

        def difference(t, lo, hi):
            col, cols, entries = slice(t, t + 1), slice(lo, hi), slice(lo // 16, hi // 16)
            nc.scalar.activation(ea[:, t, cols], b_rows[t][:].indirect(n3_t[:, entries]), ACT.Exp, bias=bias_e[:, col], scale=tau_t[:, col])
            nc.scalar.activation(ea2[:, t, cols], b_rows[t][:].indirect(n4_t[:, entries]), ACT.Exp, bias=bias_e2[:, col], scale=tau2_t[:, col])
            nc.vector.tensor_tensor(diff[:, t, cols], ea[:, t, cols], ea2[:, t, cols], ALU.subtract)
            nc.vector.tensor_scalar(z2_in[:, cols, t], diff[:, t, cols], 3.0, gm_t[:, col], ALU.mult, ALU.mult)

        for t in range(2):
            difference(t, 0, PLACES)
        for half, cols in enumerate(halves):
            for t in range(2, PACK):
                difference(t, cols.start, cols.stop)
            nc.vector.quantize_mx(
                out=z2_words[:, cols].bitcast(FP8X4), scales=z2_plane[:, cols], in_=z2_in[:, cols, :].rearrange("p j t -> p (j t)")
            )
            for t in range(PACK):
                product(h_banks[half][t], w2_dealt, w_planes[4:P, :], t, z2_words[:, cols], z2_plane[:, cols], False, True)
        for t in range(PACK):
            for half, cols in enumerate(halves):
                nc.vector.tensor_copy(h_rows[t][:, cols], h_banks[half][t][:])

        sg3 = tile("sg3", [P, PACK, PLACES], F32)
        picked = tile("picked", [P, PACK, PLACES], F32)
        kept = tile("kept", [P, PACK, PLACES], F32)
        result = tile("result", [P, PACK, PLACES], F32)
        out_rows = out_0.rearrange("(p t) j -> p t j", t=PACK)
        fetched = tile("fetched", [P, 2, PLACES], F32)
        y_in = tile("y_in", [P, PLACES, PACK], BF16)
        y_words = tile("y_words", [P, PLACES], U32)
        y_plane = tile("y_plane", [P, PLACES], U8)
        whole = [slice(0, PLACES)]
        for t in range(PACK):
            col = slice(t, t + 1)
            for cols in halves if t == 0 else whole:
                entries = slice(cols.start // 16, cols.stop // 16)
                nc.scalar.activation(
                    sg3[:, t, cols], h_rows[t][:].indirect(n6_t[:, entries]), ACT.Sigmoid, bias=bias_s3[:, col], scale=sl2_t[:, col]
                )
                if t >= 2:
                    nc.scalar.activation(fetched[:, t - 2, :], h_rows[t][:].indirect(n5_t[:]), ACT.Copy)
                nc.vector.scalar_tensor_tensor(kept[:, t, cols], sg3[:, t, cols], 1.0, h_rows[t][:, cols], ALU.subtract, ALU.mult)
                at_n5 = fetched[:, t - 2, :] if t >= 2 else h_rows[t][:].indirect(n5_t[:, entries])
                nc.vector.tensor_tensor(picked[:, t, cols], at_n5, sg3[:, t, cols], ALU.mult)
            for cols in halves if t == PACK - 1 else whole:
                nc.vector.tensor_tensor(result[:, t, cols], picked[:, t, cols], kept[:, t, cols], ALU.subtract)
            nc.sync.dma_start(out_rows[:, t, :], result[:, t, :])
        nc.scalar.copy(y_in[:, :, 0:2], result[:, 0:2, :].rearrange("p t j -> p j t"))
        for cols in halves:
            nc.vector.tensor_copy(y_in[:, cols, 2:4], result[:, 2:4, cols].rearrange("p t j -> p j t"))
        for cols in halves:
            nc.vector.quantize_mx(
                out=y_words[:, cols].bitcast(FP8X4), scales=y_plane[:, cols], in_=y_in[:, cols, :].rearrange("p j t -> p (j t)")
            )
        nc.sync.dma_start(out_1[0].rearrange("p c r -> p (c r)").bitcast(I32), y_words[:].bitcast(I32))
        for q in range(4):
            queue = nc.scalar if q % 2 == 0 else nc.sync
            queue.dma_start(out_2[0][4 * q : 4 * q + 4, :].bitcast(I32), y_plane[32 * q : 32 * q + 4, :].bitcast(I32))
